import numpy as np
import ml_dtypes


def mxq(x, axis, fmt="e4m3"):
    dtype, down = {"e4m3": (ml_dtypes.float8_e4m3fn, 7), "e5m2": (ml_dtypes.float8_e5m2, 14)}[fmt]
    v = np.moveaxis(np.asarray(x, np.float32).astype(ml_dtypes.bfloat16).astype(np.float64), axis, -1)
    blocks = v.reshape(v.shape[:-1] + (-1, 32))
    amax = np.abs(blocks).max(-1, keepdims=True)
    byte = np.maximum(np.where(amax > 0, np.frexp(amax)[1] - 1 + 127, 0) - down, 1)
    scale = np.exp2(byte - 127.0)
    codes = (blocks / scale).astype(np.float32).astype(dtype).astype(np.float64)
    return np.moveaxis((codes * scale).reshape(v.shape), -1, axis)


WIDE = False


def mx_kscale(k):
    if not WIDE:
        return np.ones(k)
    levels = np.array([10, -10, 5, -5, 0])
    if k % 512:
        return np.exp2(np.random.permutation(np.resize(levels, k // 32))).repeat(32)
    a = np.empty((k // 512, 16))
    for p in range(k // 512):
        a[p, :8] = np.random.permutation(np.resize(levels, 8))
        for g in range(8):
            far = levels[np.abs(levels - a[p, g]) >= 10]
            a[p, g + 8] = far[np.random.randint(len(far))]
    return np.exp2(a.ravel()).repeat(32)


def f64(x):
    return np.asarray(x).astype(np.float64)


def striped(idx):
    return np.tile(np.asarray(idx).reshape(-1, 16).T, (8, 1)).astype(np.uint16)


def unstriped(offs):
    return offs[:16].T.reshape(-1).astype(np.int64)


E2M1 = np.array([0.0, 0.5, 1.0, 1.5, 2.0, 3.0, 4.0, 6.0, -0.0, -0.5, -1.0, -1.5, -2.0, -3.0, -4.0, -6.0])


def pack_weight(w, fmt):
    k, n = w.shape
    w = f64(np.asarray(w, np.float32).astype(ml_dtypes.bfloat16)).reshape(k // 32, 32, n)
    amax = np.abs(w).max(1)
    if fmt == "e4m3":
        byte = np.frexp(amax)[1] - 1 + 127 - 7
    else:
        mant, ex = np.frexp(amax / 6.0)
        byte = np.where(mant > 0.5, ex, ex - 1) + 127
    byte = np.clip(np.where(amax > 0, byte, 1), 1, 254)
    scaled = (w * np.exp2(127.0 - byte)[:, None, :]).reshape(k, n).astype(np.float32)
    by_word = np.ascontiguousarray(scaled.reshape(k // 512, 128, 4, n).transpose(0, 1, 3, 2))
    if fmt == "e4m3":
        words = by_word.astype(ml_dtypes.float8_e4m3fn).view(np.uint8)
    else:
        c = by_word.astype(ml_dtypes.float4_e2m1fn).view(np.uint8) & 0xF
        words = (c[..., 0::2] | (c[..., 1::2] << 4)).reshape(k // 512, 128, 2 * n)
    return np.ascontiguousarray(words), np.ascontiguousarray(byte.astype(np.uint8).reshape(k // 512, 16, n))


def unpack_weight(words, scales, fmt):
    g, _, n = scales.shape
    words = np.ascontiguousarray(words).reshape(g, 128, n, -1)
    if fmt == "e4m3":
        vals = words.view(ml_dtypes.float8_e4m3fn).astype(np.float64)
    else:
        nib = np.empty((g, 128, n, 4), np.uint8)
        nib[..., 0::2] = words & 0xF
        nib[..., 1::2] = words >> 4
        vals = E2M1[nib]
    vals = vals * np.repeat(np.exp2(scales.astype(np.float64) - 127.0), 8, axis=1)[..., None]
    return vals.transpose(0, 1, 3, 2).reshape(g * 512, n)


def sigmoid(v):
    return 1.0 / (1.0 + np.exp(-v))


D, E, T, I, Q, G, B = 512, 512, 2048, 512, 128, 64, 8


def setup_inputs():
    n = np.random.standard_normal
    idx = np.random.permutation(T)[:I]
    fd = mx_kscale(D)
    fe = mx_kscale(E)
    keysp = pack_weight(n((D, T)) / fd[:, None], "e4m3")
    valsp = pack_weight(n((E, T)) / fe[:, None], "e4m3")
    return {
        "query": (n((D, Q)) * 0.8 / np.sqrt(D) * fd[:, None]).astype(np.float32),
        "keys_words": keysp[0],
        "keys_scales": keysp[1],
        "steep": (np.random.uniform(2.0, 8.0, (Q, 1))).astype(np.float32),
        "gout": (n((E, Q)) * 1 / np.sqrt(E) * fe[:, None]).astype(np.float32),
        "vals_words": valsp[0],
        "vals_scales": valsp[1],
        "old": (0.5 * n((Q, T))).astype(np.float32),
        "offs": striped(idx),
    }


def reference(query, keys_words, keys_scales, steep, gout, vals_words, vals_scales, old, offs):
    idx = unstriped(offs)
    keysu = unpack_weight(keys_words, keys_scales, "e4m3")
    valsu = unpack_weight(vals_words, vals_scales, "e4m3")
    queryq = mxq(f64(query), 0, "e4m3")
    keysidxg = keysu[:, idx]
    a = queryq.T @ keysidxg
    m1 = a.reshape(Q, G, I // G).mean(axis=2)
    m2 = m1.reshape(Q, B, G // B).mean(axis=2)
    mr = np.repeat(m2, G // B, axis=1)
    g1 = sigmoid((m1 - mr) * f64(steep))
    gr = np.repeat(g1, I // G, axis=1)
    p = np.exp(a) * gr
    z = np.sum(p, axis=1, keepdims=True)
    goutq = mxq(f64(gout), 0, "e4m3")
    valsidxg = valsu[:, idx]
    c0 = goutq.T @ valsidxg
    dz = np.sum(c0 * p / np.square(z) * (-1.0), axis=1, keepdims=True)
    dp = c0 / z + dz
    dgr = dp * np.exp(a)
    dg1 = dgr.reshape(Q, G, I // G).sum(axis=2)
    dmr = dg1 * g1 * (1.0 - g1) * f64(steep) * (-1.0)
    dm2 = dmr.reshape(Q, B, G // B).sum(axis=2)
    e1 = dm2 / 8.0
    r1 = np.repeat(e1, G // B, axis=1)
    dm1 = dg1 * g1 * (1.0 - g1) * f64(steep) + r1
    e2 = dm1 / 8.0
    r2 = np.repeat(e2, I // G, axis=1)
    da = dp * gr * np.exp(a) + r2
    gs = da * 512.0
    gf = np.zeros((Q, T))
    gf[:, idx] = gs
    y = f64(old) + gf
    return y

@@ -1,0 +1,161 @@
+from contextlib import ExitStack
+
+import concourse.mybir as mybir
+
+D, E, T, I, Q, G, B = 512, 512, 2048, 512, 128, 64, 8
+FLOPS = 2 * D * Q * I + 2 * E * Q * I
+
+F32 = mybir.dt.float32
+BF16 = mybir.dt.bfloat16
+I32 = mybir.dt.int32
+U32 = mybir.dt.uint32
+U16 = mybir.dt.uint16
+U8 = mybir.dt.uint8
+FP8X4 = mybir.dt.float8_e4m3fn_x4
+ALU = mybir.AluOpType
+ACT = mybir.ActivationFunctionType
+AX = mybir.AxisListType
+
+P = 128
+PACK = 4
+SLOTS = I // G
+GROUPS = G // B
+VALS_PLANE = 4
+CHUNKS = (512, 512, 512, 256, 256)
+
+
+def tile_attend_bblockcontrast_s_kernel(tc, query, keys_words, keys_scales, steep, gout, vals_words, vals_scales, old, offs, out):
+    nc = tc.nc
+    with ExitStack() as ctx:
+        pool = ctx.enter_context(tc.tile_pool(name="sb", bufs=1))
+        psum = ctx.enter_context(tc.psum_pool(name="ps", bufs=1))
+
+        offsets = pool.tile([P, I // 16], U16, name="offsets")
+        kwords = pool.tile([P, T], U32, name="kwords", align_bytes=64)
+        vwords = pool.tile([P, T], U32, name="vwords", align_bytes=64)
+        kbytes = pool.tile([P, T], U8, name="kbytes", align_bytes=64)
+        vbytes = pool.tile([P, T], U8, name="vbytes", align_bytes=64)
+        q_raw = pool.tile([P, PACK, Q], F32, name="q_raw")
+        g_raw = pool.tile([P, PACK, Q], F32, name="g_raw")
+        steep_sb = pool.tile([P, 1], F32, name="steep_sb")
+        acc = pool.tile([P, T], F32, name="acc")
+        placed = pool.tile([P, T], F32, name="placed")
+        warm = pool.tile([P, 1], F32, name="warm")
+        warm_out = pool.tile([P, 1], F32, name="warm_out")
+
+        nc.vector.memset(kbytes[:].bitcast(I32), 0)
+        nc.vector.memset(vbytes[:].bitcast(I32), 0)
+        nc.vector.memset(warm[:], 0.0)
+        nc.vector.memset(placed[:], 0.0)
+
+        def load_scales(engine, tile, scales, quad, first):
+            rows = slice(32 * quad + first, 32 * quad + first + 4)
+            engine.dma_start(out=tile[rows, :].bitcast(I32), in_=scales[0, 4 * quad : 4 * quad + 4, :].bitcast(I32))
+
+        def load_words(tile, words):
+            nc.sync.dma_start(out=tile[:].bitcast(I32), in_=words[0].rearrange("p n t -> p (n t)").bitcast(I32))
+
+        nc.sync.dma_start(offsets[:], offs)
+        nc.sync.dma_start(out=q_raw[:], in_=query.rearrange("(p j) w -> p j w", j=PACK))
+        nc.sync.dma_start(out=steep_sb[:], in_=steep)
+        for quad in range(4):
+            load_scales(nc.sync if quad < 2 else nc.scalar, kbytes, keys_scales, quad, 0)
+        load_words(kwords, keys_words)
+        for quad in range(4):
+            load_scales(nc.sync, vbytes, vals_scales, quad, VALS_PLANE)
+        nc.sync.dma_start(out=g_raw[:], in_=gout.rearrange("(p j) w -> p j w", j=PACK))
+        load_words(vwords, vals_words)
+        nc.sync.dma_start(out=acc[:], in_=old)
+
+        nc.scalar.activation(out=warm_out[:], in_=warm[:], func=ACT.Exp)
+
+        def quantize(raw, name):
+            grouped = pool.tile([P, Q, PACK], BF16, name=name + "_bf", align_bytes=64)
+            codes = pool.tile([P, Q], U32, name=name + "_codes", align_bytes=64)
+            scales = pool.tile([P, Q], U8, name=name + "_scales", align_bytes=64)
+            nc.scalar.copy(out=grouped[:], in_=raw[:].rearrange("p j w -> p w j"))
+            nc.vector.quantize_mx(out=codes[:].bitcast(FP8X4), scales=scales[:], in_=grouped[:].rearrange("p w j -> p (w j)"))
+            return codes, scales
+
+        def gather(window, dtype, name):
+            picked = pool.tile([P, I], dtype, name=name, align_bytes=64)
+            nc.vector.tensor_copy(out=picked[:], in_=window[:].indirect(offsets[:]))
+            return picked
+
+        def small(name, width):
+            return pool.tile([P, width], F32, name=name)
+
+        kb = gather(kbytes, U8, "kb")
+        q_codes, q_scales = quantize(q_raw, "q")
+        half = small("half", 1)
+        nhalf = small("nhalf", 1)
+        nc.scalar.mul(half[:], steep_sb[:], 1.0 / 16.0)
+        nc.scalar.mul(nhalf[:], steep_sb[:], -1.0 / 16.0)
+        kw = gather(kwords, U32, "kw")
+        a = psum.tile([Q, I], F32, name="a")
+        nc.tensor.matmul_mx(out=a[:], lhsT=q_codes[:].bitcast(FP8X4), lhsT_scale=q_scales[:],
+                            rhs=kw[:].bitcast(FP8X4), rhs_scale=kb[:], start=True, stop=True)
+        vb = gather(vbytes, U8, "vb")
+        g_codes, g_scales = quantize(g_raw, "g")
+
+        gsum = small("gsum", G)
+        nc.vector.tensor_reduce(out=gsum[:], in_=a[:].rearrange("p (g j) -> p g j", j=SLOTS), axis=AX.X, op=ALU.add)
+        nmax = small("nmax", 1)
+        nc.vector.tensor_reduce(out=nmax[:], in_=a[:], axis=AX.X, op=ALU.max, negate=True)
+        ea = small("ea", I)
+        nc.scalar.activation(out=ea[:], in_=a[:], func=ACT.Exp, bias=nmax[:], scale=1.0)
+        bsum = small("bsum", B)
+        nc.vector.tensor_reduce(out=bsum[:], in_=gsum[:].rearrange("p (b g) -> p b g", g=GROUPS), axis=AX.X, op=ALU.add)
+        diff = small("diff", G)
+        nc.vector.scalar_tensor_tensor(
+            out=diff[:].rearrange("p (b g) -> p b g", g=GROUPS),
+            in0=bsum[:].unsqueeze(2).to_broadcast([P, B, GROUPS]), scalar=-1.0 / GROUPS,
+            in1=gsum[:].rearrange("p (b g) -> p b g", g=GROUPS), op0=ALU.mult, op1=ALU.add)
+        th = small("th", G)
+        nc.scalar.activation(out=th[:], in_=diff[:], func=ACT.Tanh, scale=half[:])
+        slope = small("slope", G)
+        nc.scalar.activation(out=slope[:], in_=th[:], func=ACT.Identity, bias=half[:], scale=nhalf[:])
+
+        vw = gather(vwords, U32, "vw")
+        c0 = psum.tile([Q, I], F32, name="c0")
+        nc.tensor.matmul_mx(out=c0[:], lhsT=g_codes[:].bitcast(FP8X4), lhsT_scale=g_scales[:],
+                            rhs=vw[:].bitcast(FP8X4), rhs_scale=vb[VALS_PLANE:P, :], start=True, stop=True)
+
+        p = small("p", I)
+        z = small("z", 1)
+        nc.vector.scalar_tensor_tensor(
+            out=p[:].rearrange("p (g j) -> p g j", j=SLOTS),
+            in0=th[:].unsqueeze(2).to_broadcast([P, G, SLOTS]), scalar=1.0,
+            in1=ea[:].rearrange("p (g j) -> p g j", j=SLOTS), op0=ALU.add, op1=ALU.mult, accum_out=z[:])
+        rz = small("rz", 1)
+        nc.vector.reciprocal(out=rz[:], in_=z[:])
+        rz512 = small("rz512", 1)
+        nc.scalar.mul(rz512[:], rz[:], 512.0)
+        w512 = small("w512", I)
+        nc.scalar.activation(out=w512[:], in_=p[:], func=ACT.Identity, scale=rz512[:])
+
+        cw = small("cw", I)
+        s = small("s", 1)
+        nc.vector.scalar_tensor_tensor(out=cw[:], in0=c0[:], scalar=rz[:], in1=p[:], op0=ALU.mult, op1=ALU.mult, accum_out=s[:])
+        u = small("u", I)
+        nc.vector.scalar_tensor_tensor(out=u[:], in0=c0[:], scalar=s[:], in1=w512[:], op0=ALU.subtract, op1=ALU.mult)
+        ug = small("ug", G)
+        nc.vector.tensor_reduce(out=ug[:], in_=u[:].rearrange("p (g j) -> p g j", j=SLOTS), axis=AX.X, op=ALU.add)
+        h = small("h", G)
+        nc.vector.tensor_tensor(out=h[:], in0=ug[:], in1=slope[:], op=ALU.mult)
+        hb = small("hb", B)
+        nc.vector.tensor_reduce(out=hb[:], in_=h[:].rearrange("p (b g) -> p b g", g=GROUPS), axis=AX.X, op=ALU.add)
+        spread = small("spread", I)
+        nc.vector.scalar_tensor_tensor(
+            out=spread[:],
+            in0=hb[:].unsqueeze(2).to_broadcast([P, B, GROUPS * SLOTS]), scalar=-1.0 / GROUPS,
+            in1=h[:].unsqueeze(2).to_broadcast([P, G, SLOTS]),
+            op0=ALU.mult, op1=ALU.add)
+        nc.vector.tensor_tensor(out=placed[:].indirect(offsets[:]), in0=u[:], in1=spread[:], op=ALU.add)
+
+        first = 0
+        for width in CHUNKS:
+            cols = slice(first, first + width)
+            nc.vector.tensor_tensor(out=acc[:, cols], in0=acc[:, cols], in1=placed[:, cols], op=ALU.add)
+            nc.sync.dma_start(out=out[:, cols], in_=acc[:, cols])
+            first += width

@@ -1,3 +1,4 @@
+import math
 from contextlib import ExitStack
 
 import concourse.mybir as mybir
@@ -21,7 +22,10 @@ PACK = 4
 SLOTS = I // G
 GROUPS = G // B
 VALS_PLANE = 4
-CHUNKS = (512, 512, 512, 256, 256)
+HALVES = 2
+TEMPER = 8.0
+CENTRE = 25.0
+CHUNKS = (128, 384, 512, 512, 256, 256)
 
 
 def tile_attend_bblockcontrast_s_kernel(tc, query, keys_words, keys_scales, steep, gout, vals_words, vals_scales, old, offs, out):
@@ -57,7 +61,6 @@ def tile_attend_bblockcontrast_s_kernel(tc, query, keys_words, keys_scales, stee
 
         nc.sync.dma_start(offsets[:], offs)
         nc.sync.dma_start(out=q_raw[:], in_=query.rearrange("(p j) w -> p j w", j=PACK))
-        nc.sync.dma_start(out=steep_sb[:], in_=steep)
         for quad in range(4):
             load_scales(nc.sync if quad < 2 else nc.scalar, kbytes, keys_scales, quad, 0)
         load_words(kwords, keys_words)
@@ -65,6 +68,7 @@ def tile_attend_bblockcontrast_s_kernel(tc, query, keys_words, keys_scales, stee
             load_scales(nc.sync, vbytes, vals_scales, quad, VALS_PLANE)
         nc.sync.dma_start(out=g_raw[:], in_=gout.rearrange("(p j) w -> p j w", j=PACK))
         load_words(vwords, vals_words)
+        nc.sync.dma_start(out=steep_sb[:], in_=steep)
         nc.sync.dma_start(out=acc[:], in_=old)
 
         nc.scalar.activation(out=warm_out[:], in_=warm[:], func=ACT.Exp)
@@ -91,19 +95,34 @@ def tile_attend_bblockcontrast_s_kernel(tc, query, keys_words, keys_scales, stee
         nhalf = small("nhalf", 1)
         nc.scalar.mul(half[:], steep_sb[:], 1.0 / 16.0)
         nc.scalar.mul(nhalf[:], steep_sb[:], -1.0 / 16.0)
-        kw = gather(kwords, U32, "kw")
-        a = psum.tile([Q, I], F32, name="a")
-        nc.tensor.matmul_mx(out=a[:], lhsT=q_codes[:].bitcast(FP8X4), lhsT_scale=q_scales[:],
-                            rhs=kw[:].bitcast(FP8X4), rhs_scale=kb[:], start=True, stop=True)
+        halves = range(HALVES)
+        slots = [slice(k * I // HALVES, (k + 1) * I // HALVES) for k in halves]
+        groups = [slice(k * G // HALVES, (k + 1) * G // HALVES) for k in halves]
+        blocks = [slice(k * B // HALVES, (k + 1) * B // HALVES) for k in halves]
+        entries = [slice(k * I // 16 // HALVES, (k + 1) * I // 16 // HALVES) for k in halves]
+        kw = pool.tile([P, I], U32, name="kw", align_bytes=64)
+        a = [psum.tile([Q, I // HALVES], F32, name="a%d" % k) for k in halves]
+        for k in halves:
+            nc.vector.tensor_copy(out=kw[:, slots[k]], in_=kwords[:].indirect(offsets[:, entries[k]]))
+            nc.tensor.matmul_mx(out=a[k][:], lhsT=q_codes[:].bitcast(FP8X4), lhsT_scale=q_scales[:],
+                                rhs=kw[:, slots[k]].bitcast(FP8X4), rhs_scale=kb[:, slots[k]], start=True, stop=True)
         vb = gather(vbytes, U8, "vb")
         g_codes, g_scales = quantize(g_raw, "g")
+        soft = pool.tile([P, I], F32, name="soft", tag="g_raw")
+        soft_sums = small("soft_sums", HALVES)
+        for k in halves:
+            nc.scalar.activation(out=soft[:, slots[k]], in_=a[k][:], func=ACT.Exp, scale=1.0 / TEMPER, accum_out=soft_sums[:, k : k + 1])
+        soft_sum = small("soft_sum", 1)
+        nc.scalar.activation(out=soft_sum[:], in_=soft_sums[:, 0:1], func=ACT.Identity, bias=soft_sums[:, 1:2], scale=1.0)
+        nshift = small("nshift", 1)
+        nc.scalar.activation(out=nshift[:], in_=soft_sum[:].bitcast(U32), func=ACT.Copy,
+                             scale=-TEMPER * math.log(2.0) / 2.0**23, bias=TEMPER * math.log(2.0) * 127.0 + CENTRE)
 
         gsum = small("gsum", G)
-        nc.vector.tensor_reduce(out=gsum[:], in_=a[:].rearrange("p (g j) -> p g j", j=SLOTS), axis=AX.X, op=ALU.add)
-        nmax = small("nmax", 1)
-        nc.vector.tensor_reduce(out=nmax[:], in_=a[:], axis=AX.X, op=ALU.max, negate=True)
         ea = small("ea", I)
-        nc.scalar.activation(out=ea[:], in_=a[:], func=ACT.Exp, bias=nmax[:], scale=1.0)
+        for k in halves:
+            nc.vector.tensor_reduce(out=gsum[:, groups[k]], in_=a[k][:].rearrange("p (g j) -> p g j", j=SLOTS), axis=AX.X, op=ALU.add)
+            nc.scalar.activation(out=ea[:, slots[k]], in_=a[k][:], func=ACT.Exp, bias=nshift[:], scale=1.0)
         bsum = small("bsum", B)
         nc.vector.tensor_reduce(out=bsum[:], in_=gsum[:].rearrange("p (b g) -> p b g", g=GROUPS), axis=AX.X, op=ALU.add)
         diff = small("diff", G)
@@ -131,27 +150,35 @@ def tile_attend_bblockcontrast_s_kernel(tc, query, keys_words, keys_scales, stee
         nc.vector.reciprocal(out=rz[:], in_=z[:])
         rz512 = small("rz512", 1)
         nc.scalar.mul(rz512[:], rz[:], 512.0)
-        w512 = small("w512", I)
-        nc.scalar.activation(out=w512[:], in_=p[:], func=ACT.Identity, scale=rz512[:])
+        slope512 = small("slope512", G)
+        nc.scalar.activation(out=slope512[:], in_=slope[:], func=ACT.Identity, scale=rz512[:])
 
         cw = small("cw", I)
         s = small("s", 1)
         nc.vector.scalar_tensor_tensor(out=cw[:], in0=c0[:], scalar=rz[:], in1=p[:], op0=ALU.mult, op1=ALU.mult, accum_out=s[:])
-        u = small("u", I)
-        nc.vector.scalar_tensor_tensor(out=u[:], in0=c0[:], scalar=s[:], in1=w512[:], op0=ALU.subtract, op1=ALU.mult)
+
+        zu = small("zu", I)
+        u512 = small("u512", I)
         ug = small("ug", G)
-        nc.vector.tensor_reduce(out=ug[:], in_=u[:].rearrange("p (g j) -> p g j", j=SLOTS), axis=AX.X, op=ALU.add)
         h = small("h", G)
-        nc.vector.tensor_tensor(out=h[:], in0=ug[:], in1=slope[:], op=ALU.mult)
         hb = small("hb", B)
-        nc.vector.tensor_reduce(out=hb[:], in_=h[:].rearrange("p (b g) -> p b g", g=GROUPS), axis=AX.X, op=ALU.add)
         spread = small("spread", I)
-        nc.vector.scalar_tensor_tensor(
-            out=spread[:],
-            in0=hb[:].unsqueeze(2).to_broadcast([P, B, GROUPS * SLOTS]), scalar=-1.0 / GROUPS,
-            in1=h[:].unsqueeze(2).to_broadcast([P, G, SLOTS]),
-            op0=ALU.mult, op1=ALU.add)
-        nc.vector.tensor_tensor(out=placed[:].indirect(offsets[:]), in0=u[:], in1=spread[:], op=ALU.add)
+        for k in halves:
+            nc.vector.scalar_tensor_tensor(out=zu[:, slots[k]], in0=c0[:, slots[k]], scalar=s[:], in1=p[:, slots[k]], op0=ALU.subtract, op1=ALU.mult)
+            nc.scalar.activation(out=u512[:, slots[k]], in_=zu[:, slots[k]], func=ACT.Identity, scale=rz512[:])
+        for k in halves:
+            nc.vector.tensor_reduce(out=ug[:, groups[k]], in_=zu[:, slots[k]].rearrange("p (g j) -> p g j", j=SLOTS), axis=AX.X, op=ALU.add)
+        for k in halves:
+            nc.vector.tensor_tensor(out=h[:, groups[k]], in0=ug[:, groups[k]], in1=slope512[:, groups[k]], op=ALU.mult)
+        for k in halves:
+            nc.vector.tensor_reduce(out=hb[:, blocks[k]], in_=h[:, groups[k]].rearrange("p (b g) -> p b g", g=GROUPS), axis=AX.X, op=ALU.add)
+        for k in halves:
+            nc.vector.scalar_tensor_tensor(
+                out=spread[:, slots[k]],
+                in0=hb[:, blocks[k]].unsqueeze(2).to_broadcast([P, B // HALVES, GROUPS * SLOTS]), scalar=-1.0 / GROUPS,
+                in1=h[:, groups[k]].unsqueeze(2).to_broadcast([P, G // HALVES, SLOTS]),
+                op0=ALU.mult, op1=ALU.add)
+        nc.vector.tensor_tensor(out=placed[:].indirect(offsets[:]), in0=u512[:], in1=spread[:], op=ALU.add)
 
         first = 0
         for width in CHUNKS:

import math
from contextlib import ExitStack

import concourse.mybir as mybir

D, E, T, I, Q, G, B = 512, 512, 2048, 512, 128, 64, 8
FLOPS = 2 * D * Q * I + 2 * E * Q * I

F32 = mybir.dt.float32
BF16 = mybir.dt.bfloat16
I32 = mybir.dt.int32
U32 = mybir.dt.uint32
U16 = mybir.dt.uint16
U8 = mybir.dt.uint8
FP8X4 = mybir.dt.float8_e4m3fn_x4
ALU = mybir.AluOpType
ACT = mybir.ActivationFunctionType
AX = mybir.AxisListType

P = 128
PACK = 4
SLOTS = I // G
GROUPS = G // B
VALS_PLANE = 4
HALVES = 2
TEMPER = 8.0
CENTRE = 25.0
CHUNKS = (128, 384, 512, 512, 256, 256)


def tile_attend_bblockcontrast_s_kernel(tc, query, keys_words, keys_scales, steep, gout, vals_words, vals_scales, old, offs, out):
    nc = tc.nc
    with ExitStack() as ctx:
        pool = ctx.enter_context(tc.tile_pool(name="sb", bufs=1))
        psum = ctx.enter_context(tc.psum_pool(name="ps", bufs=1))

        offsets = pool.tile([P, I // 16], U16, name="offsets")
        kwords = pool.tile([P, T], U32, name="kwords", align_bytes=64)
        vwords = pool.tile([P, T], U32, name="vwords", align_bytes=64)
        kbytes = pool.tile([P, T], U8, name="kbytes", align_bytes=64)
        vbytes = pool.tile([P, T], U8, name="vbytes", align_bytes=64)
        q_raw = pool.tile([P, PACK, Q], F32, name="q_raw")
        g_raw = pool.tile([P, PACK, Q], F32, name="g_raw")
        steep_sb = pool.tile([P, 1], F32, name="steep_sb")
        acc = pool.tile([P, T], F32, name="acc")
        placed = pool.tile([P, T], F32, name="placed")
        warm = pool.tile([P, 1], F32, name="warm")
        warm_out = pool.tile([P, 1], F32, name="warm_out")

        nc.vector.memset(kbytes[:].bitcast(I32), 0)
        nc.vector.memset(vbytes[:].bitcast(I32), 0)
        nc.vector.memset(warm[:], 0.0)
        nc.vector.memset(placed[:], 0.0)

        def load_scales(engine, tile, scales, quad, first):
            rows = slice(32 * quad + first, 32 * quad + first + 4)
            engine.dma_start(out=tile[rows, :].bitcast(I32), in_=scales[0, 4 * quad : 4 * quad + 4, :].bitcast(I32))

        def load_words(tile, words):
            nc.sync.dma_start(out=tile[:].bitcast(I32), in_=words[0].rearrange("p n t -> p (n t)").bitcast(I32))

        nc.sync.dma_start(offsets[:], offs)
        nc.sync.dma_start(out=q_raw[:], in_=query.rearrange("(p j) w -> p j w", j=PACK))
        for quad in range(4):
            load_scales(nc.sync if quad < 2 else nc.scalar, kbytes, keys_scales, quad, 0)
        load_words(kwords, keys_words)
        for quad in range(4):
            load_scales(nc.sync, vbytes, vals_scales, quad, VALS_PLANE)
        nc.sync.dma_start(out=g_raw[:], in_=gout.rearrange("(p j) w -> p j w", j=PACK))
        load_words(vwords, vals_words)
        nc.sync.dma_start(out=steep_sb[:], in_=steep)
        nc.sync.dma_start(out=acc[:], in_=old)

        nc.scalar.activation(out=warm_out[:], in_=warm[:], func=ACT.Exp)

        def quantize(raw, name):
            grouped = pool.tile([P, Q, PACK], BF16, name=name + "_bf", align_bytes=64)
            codes = pool.tile([P, Q], U32, name=name + "_codes", align_bytes=64)
            scales = pool.tile([P, Q], U8, name=name + "_scales", align_bytes=64)
            nc.scalar.copy(out=grouped[:], in_=raw[:].rearrange("p j w -> p w j"))
            nc.vector.quantize_mx(out=codes[:].bitcast(FP8X4), scales=scales[:], in_=grouped[:].rearrange("p w j -> p (w j)"))
            return codes, scales

        def gather(window, dtype, name):
            picked = pool.tile([P, I], dtype, name=name, align_bytes=64)
            nc.vector.tensor_copy(out=picked[:], in_=window[:].indirect(offsets[:]))
            return picked

        def small(name, width):
            return pool.tile([P, width], F32, name=name)

        kb = gather(kbytes, U8, "kb")
        q_codes, q_scales = quantize(q_raw, "q")
        half = small("half", 1)
        nhalf = small("nhalf", 1)
        nc.scalar.mul(half[:], steep_sb[:], 1.0 / 16.0)
        nc.scalar.mul(nhalf[:], steep_sb[:], -1.0 / 16.0)
        halves = range(HALVES)
        slots = [slice(k * I // HALVES, (k + 1) * I // HALVES) for k in halves]
        groups = [slice(k * G // HALVES, (k + 1) * G // HALVES) for k in halves]
        blocks = [slice(k * B // HALVES, (k + 1) * B // HALVES) for k in halves]
        entries = [slice(k * I // 16 // HALVES, (k + 1) * I // 16 // HALVES) for k in halves]
        kw = pool.tile([P, I], U32, name="kw", align_bytes=64)
        a = [psum.tile([Q, I // HALVES], F32, name="a%d" % k) for k in halves]
        for k in halves:
            nc.vector.tensor_copy(out=kw[:, slots[k]], in_=kwords[:].indirect(offsets[:, entries[k]]))
            nc.tensor.matmul_mx(out=a[k][:], lhsT=q_codes[:].bitcast(FP8X4), lhsT_scale=q_scales[:],
                                rhs=kw[:, slots[k]].bitcast(FP8X4), rhs_scale=kb[:, slots[k]], start=True, stop=True)
        vb = gather(vbytes, U8, "vb")
        g_codes, g_scales = quantize(g_raw, "g")
        soft = pool.tile([P, I], F32, name="soft", tag="g_raw")
        soft_sums = small("soft_sums", HALVES)
        for k in halves:
            nc.scalar.activation(out=soft[:, slots[k]], in_=a[k][:], func=ACT.Exp, scale=1.0 / TEMPER, accum_out=soft_sums[:, k : k + 1])
        soft_sum = small("soft_sum", 1)
        nc.scalar.activation(out=soft_sum[:], in_=soft_sums[:, 0:1], func=ACT.Identity, bias=soft_sums[:, 1:2], scale=1.0)
        nshift = small("nshift", 1)
        nc.scalar.activation(out=nshift[:], in_=soft_sum[:].bitcast(U32), func=ACT.Copy,
                             scale=-TEMPER * math.log(2.0) / 2.0**23, bias=TEMPER * math.log(2.0) * 127.0 + CENTRE)

        gsum = small("gsum", G)
        ea = small("ea", I)
        for k in halves:
            nc.vector.tensor_reduce(out=gsum[:, groups[k]], in_=a[k][:].rearrange("p (g j) -> p g j", j=SLOTS), axis=AX.X, op=ALU.add)
            nc.scalar.activation(out=ea[:, slots[k]], in_=a[k][:], func=ACT.Exp, bias=nshift[:], scale=1.0)
        bsum = small("bsum", B)
        nc.vector.tensor_reduce(out=bsum[:], in_=gsum[:].rearrange("p (b g) -> p b g", g=GROUPS), axis=AX.X, op=ALU.add)
        diff = small("diff", G)
        nc.vector.scalar_tensor_tensor(
            out=diff[:].rearrange("p (b g) -> p b g", g=GROUPS),
            in0=bsum[:].unsqueeze(2).to_broadcast([P, B, GROUPS]), scalar=-1.0 / GROUPS,
            in1=gsum[:].rearrange("p (b g) -> p b g", g=GROUPS), op0=ALU.mult, op1=ALU.add)
        th = small("th", G)
        nc.scalar.activation(out=th[:], in_=diff[:], func=ACT.Tanh, scale=half[:])
        slope = small("slope", G)
        nc.scalar.activation(out=slope[:], in_=th[:], func=ACT.Identity, bias=half[:], scale=nhalf[:])

        vw = gather(vwords, U32, "vw")
        c0 = psum.tile([Q, I], F32, name="c0")
        nc.tensor.matmul_mx(out=c0[:], lhsT=g_codes[:].bitcast(FP8X4), lhsT_scale=g_scales[:],
                            rhs=vw[:].bitcast(FP8X4), rhs_scale=vb[VALS_PLANE:P, :], start=True, stop=True)

        p = small("p", I)
        z = small("z", 1)
        nc.vector.scalar_tensor_tensor(
            out=p[:].rearrange("p (g j) -> p g j", j=SLOTS),
            in0=th[:].unsqueeze(2).to_broadcast([P, G, SLOTS]), scalar=1.0,
            in1=ea[:].rearrange("p (g j) -> p g j", j=SLOTS), op0=ALU.add, op1=ALU.mult, accum_out=z[:])
        rz = small("rz", 1)
        nc.vector.reciprocal(out=rz[:], in_=z[:])
        rz512 = small("rz512", 1)
        nc.scalar.mul(rz512[:], rz[:], 512.0)
        slope512 = small("slope512", G)
        nc.scalar.activation(out=slope512[:], in_=slope[:], func=ACT.Identity, scale=rz512[:])

        cw = small("cw", I)
        s = small("s", 1)
        nc.vector.scalar_tensor_tensor(out=cw[:], in0=c0[:], scalar=rz[:], in1=p[:], op0=ALU.mult, op1=ALU.mult, accum_out=s[:])

        zu = small("zu", I)
        u512 = small("u512", I)
        ug = small("ug", G)
        h = small("h", G)
        hb = small("hb", B)
        spread = small("spread", I)
        for k in halves:
            nc.vector.scalar_tensor_tensor(out=zu[:, slots[k]], in0=c0[:, slots[k]], scalar=s[:], in1=p[:, slots[k]], op0=ALU.subtract, op1=ALU.mult)
            nc.scalar.activation(out=u512[:, slots[k]], in_=zu[:, slots[k]], func=ACT.Identity, scale=rz512[:])
        for k in halves:
            nc.vector.tensor_reduce(out=ug[:, groups[k]], in_=zu[:, slots[k]].rearrange("p (g j) -> p g j", j=SLOTS), axis=AX.X, op=ALU.add)
        for k in halves:
            nc.vector.tensor_tensor(out=h[:, groups[k]], in0=ug[:, groups[k]], in1=slope512[:, groups[k]], op=ALU.mult)
        for k in halves:
            nc.vector.tensor_reduce(out=hb[:, blocks[k]], in_=h[:, groups[k]].rearrange("p (b g) -> p b g", g=GROUPS), axis=AX.X, op=ALU.add)
        for k in halves:
            nc.vector.scalar_tensor_tensor(
                out=spread[:, slots[k]],
                in0=hb[:, blocks[k]].unsqueeze(2).to_broadcast([P, B // HALVES, GROUPS * SLOTS]), scalar=-1.0 / GROUPS,
                in1=h[:, groups[k]].unsqueeze(2).to_broadcast([P, G // HALVES, SLOTS]),
                op0=ALU.mult, op1=ALU.add)
        nc.vector.tensor_tensor(out=placed[:].indirect(offsets[:]), in0=u512[:], in1=spread[:], op=ALU.add)

        first = 0
        for width in CHUNKS:
            cols = slice(first, first + width)
            nc.vector.tensor_tensor(out=acc[:, cols], in0=acc[:, cols], in1=placed[:, cols], op=ALU.add)
            nc.sync.dma_start(out=out[:, cols], in_=acc[:, cols])
            first += width
